import numpy as np
import ml_dtypes


def mxq(x, axis, fmt="e4m3"):
    dtype, down = {"e4m3": (ml_dtypes.float8_e4m3fn, 7), "e5m2": (ml_dtypes.float8_e5m2, 14)}[fmt]
    v = np.moveaxis(np.asarray(x, np.float32).astype(ml_dtypes.bfloat16).astype(np.float64), axis, -1)
    blocks = v.reshape(v.shape[:-1] + (-1, 32))
    amax = np.abs(blocks).max(-1, keepdims=True)
    byte = np.maximum(np.where(amax > 0, np.frexp(amax)[1] - 1 + 127, 0) - down, 1)
    scale = np.exp2(byte - 127.0)
    codes = (blocks / scale).astype(np.float32).astype(dtype).astype(np.float64)
    return np.moveaxis((codes * scale).reshape(v.shape), -1, axis)


WIDE = False


def mx_kscale(k):
    if not WIDE:
        return np.ones(k)
    levels = np.array([10, -10, 5, -5, 0])
    if k % 512:
        return np.exp2(np.random.permutation(np.resize(levels, k // 32))).repeat(32)
    a = np.empty((k // 512, 16))
    for p in range(k // 512):
        a[p, :8] = np.random.permutation(np.resize(levels, 8))
        for g in range(8):
            far = levels[np.abs(levels - a[p, g]) >= 10]
            a[p, g + 8] = far[np.random.randint(len(far))]
    return np.exp2(a.ravel()).repeat(32)


def f64(x):
    return np.asarray(x).astype(np.float64)


def striped(idx):
    return np.tile(idx.reshape(-1, 16).T, (8, 1)).astype(np.uint16)


def unstriped(offs):
    return offs[:16].T.reshape(-1).astype(np.int64)


def striped8(idx):
    return np.concatenate([x.reshape(-1, 16).T for x in idx]).astype(np.uint16)


def runs(offs, k):
    lists = np.stack([offs[16 * r : 16 * r + 16].T.reshape(-1) for r in range(8)]).astype(np.int64)
    return lists[np.arange(k) % 512 // 64]


def pack_weight(w):
    k, n = w.shape
    w = f64(np.asarray(w, np.float32).astype(ml_dtypes.bfloat16)).reshape(k // 32, 32, n)
    amax = np.abs(w).max(1)
    byte = np.clip(np.where(amax > 0, np.frexp(amax)[1] - 1 + 127 - 7, 1), 1, 254)
    scaled = (w * np.exp2(127.0 - byte)[:, None, :]).reshape(k, n).astype(np.float32)
    words = np.ascontiguousarray(scaled.reshape(k // 512, 128, 4, n).transpose(0, 1, 3, 2)).astype(ml_dtypes.float8_e4m3fn).view(np.uint8)
    return words, np.ascontiguousarray(byte.astype(np.uint8).reshape(k // 512, 16, n))


def unpack_weight(words, scales):
    g, p, n, _ = words.shape
    vals = np.ascontiguousarray(words).view(ml_dtypes.float8_e4m3fn).astype(np.float64) * np.repeat(np.exp2(scales.astype(np.float64) - 127.0), 8, axis=1)[..., None]
    return vals.transpose(0, 1, 3, 2).reshape(g * 512, n)

def planes(y):
    n, m = y.shape
    v = y.astype(np.float32).astype(ml_dtypes.bfloat16).astype(np.float64).reshape(n // 32, 32, m)
    top = np.abs(v).max(1)
    byte = np.clip(np.where(top > 0, np.frexp(top)[1] - 1 + 127 - 7, 1), 1, 254)
    codes = (v * np.exp2(127.0 - byte)[:, None, :]).reshape(n, m).astype(np.float32).astype(ml_dtypes.float8_e4m3fn).view(np.uint8)
    words = codes.reshape(n // 512, 128, 4, m).transpose(0, 1, 3, 2)
    return np.ascontiguousarray(words), np.ascontiguousarray(byte.astype(np.uint8).reshape(n // 512, 16, m))


K, T, S, G, H = 512, 1024, 512, 2048, 512


def setup_inputs():
    n = np.random.standard_normal
    s = mx_kscale(K)[:, None]
    packed_xT = pack_weight(n((K, T)) * s)
    packed_dT = pack_weight(n((K, G)) / s)
    return {
        "x_words": packed_xT[0],
        "x_scales": packed_xT[1],
        "d_words": packed_dT[0],
        "d_scales": packed_dT[1],
        "gs": (np.random.uniform(0.5, 1.5, (K, 1)) * s).astype(np.float32),
        "offs": striped(np.random.permutation(T)[:S]),
        "k1": striped8(np.random.randint(0, G, (8, H))),
        "n1": striped8(np.stack([np.random.permutation(S) for _ in range(8)])),
        "n2": striped8(np.stack([np.random.permutation(S) for _ in range(8)])),
        "k2": striped8(np.random.randint(0, G, (8, H))),
        "n3": striped8(np.stack([np.random.permutation(S) for _ in range(8)])),
        "n4": striped8(np.stack([np.random.permutation(S) for _ in range(8)])),
        "n5": striped8(np.stack([np.random.permutation(S) for _ in range(8)])),
    }


def reference(x_words, x_scales, d_words, d_scales, gs, offs, k1, n1, n2, k2, n3, n4, n5):
    d_k2 = unpack_weight(d_words, d_scales)[np.arange(K)[:, None], runs(k2, K)]
    d_k1 = unpack_weight(d_words, d_scales)[np.arange(K)[:, None], runs(k1, K)]
    xq = unpack_weight(x_words, x_scales)[:, unstriped(offs)]
    h = 0.0625 * (d_k1.T @ xq)
    z = f64(gs) * (np.maximum(h[np.arange(H)[:, None], runs(n1, H)], h[np.arange(H)[:, None], runs(n2, H)]) - (0.75 * h))
    h2 = 0.0625 * ((d_k2.T @ mxq(z, 0, "e4m3")))
    ex = np.exp(0.5 * h2)
    out_0 = np.log((ex + ex[np.arange(H)[:, None], runs(n3, H)]) / (ex[np.arange(H)[:, None], runs(n4, H)] + ex[np.arange(H)[:, None], runs(n5, H)]))
    return (out_0,) + planes(out_0)

@@ -1,0 +1,178 @@
+from contextlib import ExitStack
+
+import concourse.mybir as mybir
+
+F32 = mybir.dt.float32
+BF16 = mybir.dt.bfloat16
+I32 = mybir.dt.int32
+U32 = mybir.dt.uint32
+U16 = mybir.dt.uint16
+U8 = mybir.dt.uint8
+FP8X4 = mybir.dt.float8_e4m3fn_x4
+ALU = mybir.AluOpType
+ACT = mybir.ActivationFunctionType
+
+P = 128
+PACK = 4
+K, T, S, G, H = 512, 1024, 512, 2048, 512
+CH = 256
+NCH = S // CH
+LCOL = CH // 16
+SCALAR_TILES = (0, 1, 2, 3)
+FLOPS = 2 * 2 * K * H * S
+
+
+def tile_picked_codeoverodds_none_po_kernel(tc, x_words, x_scales, d_words, d_scales, gs, offs, k1, n1, n2, k2, n3, n4, n5, out_0, out_1, out_2):
+    nc = tc.nc
+    with ExitStack() as ctx:
+        keep = ctx.enter_context(tc.tile_pool(name="keep", bufs=1))
+        ring = ctx.enter_context(tc.tile_pool(name="ring", bufs=3))
+        psum = ctx.enter_context(tc.psum_pool(name="psum", bufs=1))
+
+        def load_list(name, src):
+            lt = keep.tile([P, S // 16], U16, name=name)
+            nc.sync.dma_start(lt[:], src)
+            return lt
+
+        dsc = keep.tile([P, G], U8, name="dsc", align_bytes=64)
+        xsc = keep.tile([P, T], U8, name="xsc", align_bytes=64)
+
+        k1_t = load_list("k1_t", k1)
+        d_rows = d_scales[0].bitcast(I32).rearrange("(g e) c -> e g c", e=2)
+        for e in range(2):
+            nc.scalar.dma_start(dsc[e:P:2, :].bitcast(I32), d_rows[e].unsqueeze(1).to_broadcast([8, 8, G // 4]))
+        offs_t = load_list("offs_t", offs)
+        xw = keep.tile([P, T], I32, name="xw", align_bytes=64)
+        nc.sync.dma_start(xw[:], x_words[0].rearrange("p n t -> p (n t)").bitcast(I32))
+        dw = keep.tile([P, G], I32, name="dw", align_bytes=64)
+        nc.sync.dma_start(dw[:], d_words[0].rearrange("p n t -> p (n t)").bitcast(I32))
+        x_rows = x_scales[0].bitcast(I32).rearrange("(q r) c -> r q c", r=4)
+        for r in range(4):
+            queue = nc.scalar if r < 2 else nc.gpsimd
+            queue.dma_start(xsc[r:P:4, :].bitcast(I32), x_rows[r].unsqueeze(1).to_broadcast([4, 8, T // 4]))
+        gs_t = keep.tile([P, PACK], F32, name="gs_t")
+        nc.gpsimd.dma_start(gs_t[:], gs.rearrange("(p t) o -> p (t o)", t=PACK))
+        k2_t = load_list("k2_t", k2)
+        n1_t = load_list("n1_t", n1)
+        n2_t = load_list("n2_t", n2)
+        n3_t = load_list("n3_t", n3)
+        n4_t = load_list("n4_t", n4)
+        n5_t = load_list("n5_t", n5)
+
+        def pick_scales(name, lt, queue):
+            got = keep.tile([P, H], U8, name=name + "_got", align_bytes=64)
+            nc.vector.tensor_copy(got[:], dsc[:].indirect(lt[:]))
+            dealt = keep.tile([P, H], U8, name=name, align_bytes=64)
+            nc.vector.tensor_copy(
+                dealt[:].rearrange("p (t m) -> p m t", t=PACK), got[:].rearrange("p (m t) -> p m t", t=PACK)
+            )
+            for e in range(2):
+                queue.dma_start(dealt[2 + e : P : 32, :].bitcast(I32), dealt[16 + e : P : 32, :].bitcast(I32))
+            return dealt
+
+        def pick_words(name, lt):
+            got = keep.tile([P, H], U32, name=name + "_got", align_bytes=64)
+            nc.vector.tensor_copy(got[:], dw[:].bitcast(U32).indirect(lt[:]))
+            dealt = keep.tile([P, H], U32, name=name, align_bytes=64)
+            nc.vector.tensor_copy(
+                dealt[:].rearrange("p (t m) -> p m t", t=PACK), got[:].rearrange("p (m t) -> p m t", t=PACK)
+            )
+            return dealt
+
+        d1s = pick_scales("d1s", k1_t, nc.scalar)
+        xg = keep.tile([P, S], U32, name="xg", align_bytes=64)
+        nc.vector.tensor_copy(xg[:], xw[:].bitcast(U32).indirect(offs_t[:]))
+        xs = keep.tile([P, S], U8, name="xs", align_bytes=64)
+        nc.vector.tensor_copy(xs[:], xsc[:].indirect(offs_t[:]))
+        d1w = pick_words("d1w", k1_t)
+        gw = keep.tile([P, PACK], F32, name="gw")
+        nc.gpsimd.tensor_scalar(gw[:], gs_t[:], 0.75 * 0.0625, 0.0, ALU.mult, ALU.add)
+
+        h = []
+        w = []
+        for t in range(PACK):
+            acc = psum.tile([P, S], F32, name=f"bank{t}", tag=f"bank{t}")
+            cols = slice(P * t, P * (t + 1))
+            nc.tensor.matmul_mx(out=acc[:], lhsT=d1w[:, cols].bitcast(FP8X4), lhsT_scale=d1s[:, cols],
+                                rhs=xg[:].bitcast(FP8X4), rhs_scale=xs[:], start=True, stop=True)
+            ht = keep.tile([P, S], F32, name=f"h{t}")
+            nc.scalar.activation(ht[:], acc[:], ACT.Copy, scale=0.0625)
+            wt = keep.tile([P, S], F32, name=f"w{t}")
+            nc.scalar.activation(wt[:], acc[:], ACT.Copy, scale=gw[:, t : t + 1])
+            h.append(ht)
+            w.append(wt)
+
+        d2s = pick_scales("d2s", k2_t, nc.sync)
+        d2w = pick_words("d2w", k2_t)
+
+        ex = [keep.tile([P, S], F32, name=f"ex{t}") for t in range(PACK)]
+        h2 = [keep.tile([P, S], F32, name=f"h2_{t}") for t in SCALAR_TILES]
+        for c in range(NCH):
+            cols = slice(CH * c, CH * (c + 1))
+            lcols = slice(LCOL * c, LCOL * (c + 1))
+            zb = keep.tile([P, PACK, CH], BF16, name=f"zb{c}", align_bytes=64)
+            for t in range(PACK):
+                a = ring.tile([P, CH], F32, name="a")
+                nc.vector.tensor_copy(a[:], h[t][:].indirect(n1_t[:, lcols]))
+                b = ring.tile([P, CH], F32, name="b")
+                nc.vector.tensor_copy(b[:], h[t][:].indirect(n2_t[:, lcols]))
+                m = ring.tile([P, CH], F32, name="m")
+                nc.vector.tensor_tensor(m[:], a[:], b[:], ALU.max)
+                nc.vector.scalar_tensor_tensor(zb[:, t, :], m[:], gs_t[:, t : t + 1], w[t][:, cols], ALU.mult, ALU.subtract)
+            zi = keep.tile([P, CH * PACK], BF16, name=f"zi{c}", align_bytes=64)
+            eng_copy = nc.scalar.copy if c == 0 else nc.vector.tensor_copy
+            eng_copy(zi[:].rearrange("p (c i t) -> p c t i", i=4, t=PACK), zb[:].rearrange("p t (c i) -> p c t i", i=4))
+            zq = keep.tile([P, CH], U32, name=f"zq{c}", align_bytes=64)
+            zs = keep.tile([P, CH], U8, name=f"zs{c}", align_bytes=64)
+            nc.vector.quantize_mx(out=zq[:].bitcast(FP8X4), scales=zs[:], in_=zi[:])
+            for t in range(PACK):
+                bank = (PACK * (c + 1) + t) % 8
+                acc = psum.tile([P, S], F32, name=f"bank{bank}", tag=f"bank{bank}")
+                mcols = slice(P * t, P * (t + 1))
+                nc.tensor.matmul_mx(out=acc[:, :CH], lhsT=d2w[:, mcols].bitcast(FP8X4), lhsT_scale=d2s[:, mcols],
+                                    rhs=zq[:].bitcast(FP8X4), rhs_scale=zs[:], start=True, stop=True)
+                nc.scalar.activation(ex[t][:, cols], acc[:, :CH], ACT.Exp, scale=0.03125)
+                if t in SCALAR_TILES:
+                    nc.scalar.activation(h2[t][:, cols], acc[:, :CH], ACT.Copy, scale=0.03125)
+
+        g4 = {}
+        for c in range(NCH):
+            lcols = slice(LCOL * c, LCOL * (c + 1))
+            for t in SCALAR_TILES:
+                g4[c, t] = keep.tile([P, CH], F32, name=f"g4_{c}_{t}")
+                nc.scalar.activation(g4[c, t][:], h2[t][:].indirect(n4_t[:, lcols]), ACT.Exp)
+
+        nd = {}
+        for c in range(NCH):
+            cols = slice(CH * c, CH * (c + 1))
+            lcols = slice(LCOL * c, LCOL * (c + 1))
+            for t in range(PACK):
+                nd[c, t] = keep.tile([P, 2, CH], F32, name=f"nd{c}_{t}")
+                g3 = ring.tile([P, CH], F32, name="g3")
+                nc.vector.tensor_copy(g3[:], ex[t][:].indirect(n3_t[:, lcols]))
+                if t not in SCALAR_TILES:
+                    g4[c, t] = keep.tile([P, CH], F32, name=f"g4_{c}_{t}")
+                    nc.vector.tensor_copy(g4[c, t][:], ex[t][:].indirect(n4_t[:, lcols]))
+                nc.vector.tensor_tensor(nd[c, t][:, 1, :], ex[t][:].indirect(n5_t[:, lcols]), g4[c, t][:], ALU.add)
+                nc.vector.tensor_tensor(nd[c, t][:, 0, :], g3[:], ex[t][:, cols], ALU.add)
+
+        oq = keep.tile([P, S], U32, name="oq", align_bytes=64)
+        osc = keep.tile([P, S], U8, name="osc", align_bytes=64)
+        out_rows = out_0.rearrange("(p t) j -> p t j", t=PACK)
+        words_out = out_1[0].rearrange("p n t -> p (n t)").bitcast(I32)
+        for c in range(NCH):
+            cols = slice(CH * c, CH * (c + 1))
+            y = keep.tile([P, PACK, CH], F32, name=f"y{c}")
+            for t in range(PACK):
+                ln = ring.tile([P, 2, CH], F32, name="ln")
+                nc.scalar.activation(ln[:], nd[c, t][:], ACT.Ln)
+                nc.vector.tensor_tensor(y[:, t, :], ln[:, 0, :], ln[:, 1, :], ALU.subtract)
+            nc.sync.dma_start(out_rows[:, :, cols], y[:])
+            yi = keep.tile([P, CH * PACK], BF16, name=f"yi{c}", align_bytes=64)
+            nc.vector.tensor_copy(yi[:].rearrange("p (c i t) -> p c t i", i=4, t=PACK), y[:].rearrange("p t (c i) -> p c t i", i=4))
+            nc.vector.quantize_mx(out=oq[:, cols].bitcast(FP8X4), scales=osc[:, cols], in_=yi[:])
+            nc.sync.dma_start(words_out[:, cols], oq[:, cols].bitcast(I32))
+        scales_out = out_2[0].bitcast(I32).rearrange("(q r) c -> r q c", r=4)
+        for r in range(4):
+            queue = nc.scalar if r % 2 else nc.sync
+            queue.dma_start(scales_out[r], osc[r:P:32, :].bitcast(I32))

@@ -1,6 +1,7 @@
 from contextlib import ExitStack
 
 import concourse.mybir as mybir
+from concourse.masks import make_identity
 
 F32 = mybir.dt.float32
 BF16 = mybir.dt.bfloat16
@@ -15,10 +16,10 @@ ACT = mybir.ActivationFunctionType
 P = 128
 PACK = 4
 K, T, S, G, H = 512, 1024, 512, 2048, 512
-CH = 256
-NCH = S // CH
-LCOL = CH // 16
-SCALAR_TILES = (0, 1, 2, 3)
+Z_CHUNKS = ((0, 384), (384, 512))
+Z_PIECES = (((0, 256), (256, 384)), ((384, 512),))
+HELD = {("b", (1, 2)): "zi0", ("b", (1, 3)): "zi256"}
+OUT_CHUNKS = ((0, 256), (256, 512))
 FLOPS = 2 * 2 * K * H * S
 
 
@@ -35,7 +36,7 @@ def tile_picked_codeoverodds_none_po_kernel(tc, x_words, x_scales, d_words, d_sc
             return lt
 
         dsc = keep.tile([P, G], U8, name="dsc", align_bytes=64)
-        xsc = keep.tile([P, T], U8, name="xsc", align_bytes=64)
+        xsc = keep.tile([P, T], U8, name="xsc", tag="xsc", align_bytes=64)
 
         k1_t = load_list("k1_t", k1)
         d_rows = d_scales[0].bitcast(I32).rearrange("(g e) c -> e g c", e=2)
@@ -59,8 +60,8 @@ def tile_picked_codeoverodds_none_po_kernel(tc, x_words, x_scales, d_words, d_sc
         n4_t = load_list("n4_t", n4)
         n5_t = load_list("n5_t", n5)
 
-        def pick_scales(name, lt, queue):
-            got = keep.tile([P, H], U8, name=name + "_got", align_bytes=64)
+        def pick_scales(name, lt, queue, tag):
+            got = keep.tile([P, H], U8, name=name + "_got", tag=tag, align_bytes=64)
             nc.vector.tensor_copy(got[:], dsc[:].indirect(lt[:]))
             dealt = keep.tile([P, H], U8, name=name, align_bytes=64)
             nc.vector.tensor_copy(
@@ -70,8 +71,8 @@ def tile_picked_codeoverodds_none_po_kernel(tc, x_words, x_scales, d_words, d_sc
                 queue.dma_start(dealt[2 + e : P : 32, :].bitcast(I32), dealt[16 + e : P : 32, :].bitcast(I32))
             return dealt
 
-        def pick_words(name, lt):
-            got = keep.tile([P, H], U32, name=name + "_got", align_bytes=64)
+        def pick_words(name, lt, tag):
+            got = keep.tile([P, H], U32, name=name + "_got", tag=tag, align_bytes=64)
             nc.vector.tensor_copy(got[:], dw[:].bitcast(U32).indirect(lt[:]))
             dealt = keep.tile([P, H], U32, name=name, align_bytes=64)
             nc.vector.tensor_copy(
@@ -79,12 +80,14 @@ def tile_picked_codeoverodds_none_po_kernel(tc, x_words, x_scales, d_words, d_sc
             )
             return dealt
 
-        d1s = pick_scales("d1s", k1_t, nc.scalar)
+        d1s = pick_scales("d1s", k1_t, nc.scalar, "d1s_got")
         xg = keep.tile([P, S], U32, name="xg", align_bytes=64)
         nc.vector.tensor_copy(xg[:], xw[:].bitcast(U32).indirect(offs_t[:]))
         xs = keep.tile([P, S], U8, name="xs", align_bytes=64)
         nc.vector.tensor_copy(xs[:], xsc[:].indirect(offs_t[:]))
-        d1w = pick_words("d1w", k1_t)
+        d1w = pick_words("d1w", k1_t, "d1w_got")
+        ident = keep.tile([P, P], F32, name="ident")
+        make_identity(nc, ident[:])
         gw = keep.tile([P, PACK], F32, name="gw")
         nc.gpsimd.tensor_scalar(gw[:], gs_t[:], 0.75 * 0.0625, 0.0, ALU.mult, ALU.add)
 
@@ -102,76 +105,138 @@ def tile_picked_codeoverodds_none_po_kernel(tc, x_words, x_scales, d_words, d_sc
             h.append(ht)
             w.append(wt)
 
-        d2s = pick_scales("d2s", k2_t, nc.sync)
-        d2w = pick_words("d2w", k2_t)
+        d2s = pick_scales("d2s", k2_t, nc.sync, "xsc")
+        d2w = pick_words("d2w", k2_t, "d1w_got")
+
+        def listed(lt, lo, hi):
+            return lt[:, lo // 16 : hi // 16]
 
         ex = [keep.tile([P, S], F32, name=f"ex{t}") for t in range(PACK)]
-        h2 = [keep.tile([P, S], F32, name=f"h2_{t}") for t in SCALAR_TILES]
-        for c in range(NCH):
-            cols = slice(CH * c, CH * (c + 1))
-            lcols = slice(LCOL * c, LCOL * (c + 1))
-            zb = keep.tile([P, PACK, CH], BF16, name=f"zb{c}", align_bytes=64)
+        h2 = [keep.tile([P, S], F32, name=f"h2_{t}") for t in range(PACK)]
+        zb = [keep.tile([P, PACK, hi - lo], BF16, name=f"zb{lo}", align_bytes=64) for lo, hi in Z_CHUNKS]
+        units = [(c, t) for c in range(len(Z_CHUNKS)) for t in range(PACK)]
+        a, b, m = {}, {}, {}
+
+        def fetch(store, name, lt, u):
+            lo, hi = Z_CHUNKS[u[0]]
+            if (name, u) in HELD:
+                store[u] = keep.tile([P, hi - lo], F32, name=name + "_held", tag=HELD[name, u], align_bytes=64)
+            else:
+                store[u] = ring.tile([P, hi - lo], F32, name=name)
+            nc.vector.tensor_copy(store[u][:], h[u[1]][:].indirect(listed(lt, lo, hi)))
+
+        def larger(u):
+            lo, hi = Z_CHUNKS[u[0]]
+            m[u] = ring.tile([P, hi - lo], F32, name="m")
+            nc.vector.tensor_tensor(m[u][:], a[u][:], b[u][:], ALU.max)
+
+        def weigh(u):
+            c, t = u
+            lo, hi = Z_CHUNKS[c]
+            nc.vector.scalar_tensor_tensor(zb[c][:, t, :], m[u][:], gs_t[:, t : t + 1], w[t][:, lo:hi], ALU.mult, ALU.subtract)
+
+        def interleave(copy, dst, src):
+            copy(dst.rearrange("p (c i t) -> p c t i", i=4, t=PACK), src.rearrange("p t (c i) -> p c t i", i=4))
+
+        def second_product(c):
+            last = c == len(Z_CHUNKS) - 1
+            base = Z_CHUNKS[c][0]
+            first_bank = 0 if last else PACK
+            acc2 = [psum.tile([P, S], F32, name=f"bank{first_bank + t}", tag=f"bank{first_bank + t}") for t in range(PACK)]
+            for lo, hi in Z_PIECES[c]:
+                zi = keep.tile([P, (hi - lo) * PACK], BF16, name=f"zi{lo}", tag=f"zi{lo}", align_bytes=64)
+                interleave(nc.vector.tensor_copy if last else nc.scalar.copy, zi[:], zb[c][:, :, lo - base : hi - base])
+                zq = keep.tile([P, hi - lo], U32, name=f"zq{lo}", align_bytes=64)
+                zs = keep.tile([P, hi - lo], U8, name=f"zs{lo}", align_bytes=64)
+                nc.vector.quantize_mx(out=zq[:].bitcast(FP8X4), scales=zs[:], in_=zi[:])
+                for t in range(PACK):
+                    mcols = slice(P * t, P * (t + 1))
+                    nc.tensor.matmul_mx(out=acc2[t][:, lo:hi], lhsT=d2w[:, mcols].bitcast(FP8X4), lhsT_scale=d2s[:, mcols],
+                                        rhs=zq[:].bitcast(FP8X4), rhs_scale=zs[:], start=True, stop=True)
+            lo, hi = Z_CHUNKS[c]
             for t in range(PACK):
-                a = ring.tile([P, CH], F32, name="a")
-                nc.vector.tensor_copy(a[:], h[t][:].indirect(n1_t[:, lcols]))
-                b = ring.tile([P, CH], F32, name="b")
-                nc.vector.tensor_copy(b[:], h[t][:].indirect(n2_t[:, lcols]))
-                m = ring.tile([P, CH], F32, name="m")
-                nc.vector.tensor_tensor(m[:], a[:], b[:], ALU.max)
-                nc.vector.scalar_tensor_tensor(zb[:, t, :], m[:], gs_t[:, t : t + 1], w[t][:, cols], ALU.mult, ALU.subtract)
-            zi = keep.tile([P, CH * PACK], BF16, name=f"zi{c}", align_bytes=64)
-            eng_copy = nc.scalar.copy if c == 0 else nc.vector.tensor_copy
-            eng_copy(zi[:].rearrange("p (c i t) -> p c t i", i=4, t=PACK), zb[:].rearrange("p t (c i) -> p c t i", i=4))
-            zq = keep.tile([P, CH], U32, name=f"zq{c}", align_bytes=64)
-            zs = keep.tile([P, CH], U8, name=f"zs{c}", align_bytes=64)
-            nc.vector.quantize_mx(out=zq[:].bitcast(FP8X4), scales=zs[:], in_=zi[:])
+                nc.scalar.activation(ex[t][:, lo:hi], acc2[t][:, lo:hi], ACT.Exp, scale=0.03125)
+            return acc2
+
+        def raw_second(acc2, c, t, on_vector):
+            lo, hi = Z_CHUNKS[c]
+            if on_vector:
+                nc.vector.tensor_scalar_mul(h2[t][:, lo:hi], acc2[t][:, lo:hi], 0.03125)
+            else:
+                nc.scalar.activation(h2[t][:, lo:hi], acc2[t][:, lo:hi], ACT.Copy, scale=0.03125)
+
+        fetch(a, "a", n1_t, units[0])
+        fetch(b, "b", n2_t, units[0])
+        for u, ahead in zip(units, units[1:] + [None]):
+            if ahead:
+                fetch(a, "a", n1_t, ahead)
+            larger(u)
+            if ahead:
+                fetch(b, "b", n2_t, ahead)
+            weigh(u)
+            if u == (0, PACK - 1):
+                early = second_product(0)
+                raw_second(early, 0, 0, False)
+                raw_second(early, 0, 1, False)
+        late = second_product(1)
+        raw_second(early, 0, 2, True)
+        raw_second(early, 0, 3, True)
+        for t in range(PACK):
+            raw_second(late, 1, t, False)
+
+        g3 = [keep.tile([P, S], F32, name=f"g3_{t}") for t in range(PACK)]
+        for lo in range(0, S, 256):
             for t in range(PACK):
-                bank = (PACK * (c + 1) + t) % 8
-                acc = psum.tile([P, S], F32, name=f"bank{bank}", tag=f"bank{bank}")
+                nc.scalar.activation(g3[t][:, lo : lo + 256], h2[t][:].indirect(listed(n3_t, lo, lo + 256)), ACT.Exp)
+
+        num_t = []
+        for jb in range(S // P):
+            bank = psum.tile([P, S], F32, name=f"bank{jb}", tag=f"bank{jb}")
+            jcols = slice(P * jb, P * (jb + 1))
+            for t in range(PACK):
                 mcols = slice(P * t, P * (t + 1))
-                nc.tensor.matmul_mx(out=acc[:, :CH], lhsT=d2w[:, mcols].bitcast(FP8X4), lhsT_scale=d2s[:, mcols],
-                                    rhs=zq[:].bitcast(FP8X4), rhs_scale=zs[:], start=True, stop=True)
-                nc.scalar.activation(ex[t][:, cols], acc[:, :CH], ACT.Exp, scale=0.03125)
-                if t in SCALAR_TILES:
-                    nc.scalar.activation(h2[t][:, cols], acc[:, :CH], ACT.Copy, scale=0.03125)
+                nc.tensor.matmul(bank[:, mcols], ex[t][:, jcols], ident[:], start=True, stop=False, is_transpose=True)
+                nc.tensor.matmul(bank[:, mcols], g3[t][:, jcols], ident[:], start=False, stop=True, is_transpose=True)
+            num_t.append(bank)
 
+        den = {}
         g4 = {}
-        for c in range(NCH):
-            lcols = slice(LCOL * c, LCOL * (c + 1))
-            for t in SCALAR_TILES:
-                g4[c, t] = keep.tile([P, CH], F32, name=f"g4_{c}_{t}")
-                nc.scalar.activation(g4[c, t][:], h2[t][:].indirect(n4_t[:, lcols]), ACT.Exp)
+        pieces = [(lo, hi, t) for lo, hi in OUT_CHUNKS for t in range(PACK)]
 
-        nd = {}
-        for c in range(NCH):
-            cols = slice(CH * c, CH * (c + 1))
-            lcols = slice(LCOL * c, LCOL * (c + 1))
-            for t in range(PACK):
-                nd[c, t] = keep.tile([P, 2, CH], F32, name=f"nd{c}_{t}")
-                g3 = ring.tile([P, CH], F32, name="g3")
-                nc.vector.tensor_copy(g3[:], ex[t][:].indirect(n3_t[:, lcols]))
-                if t not in SCALAR_TILES:
-                    g4[c, t] = keep.tile([P, CH], F32, name=f"g4_{c}_{t}")
-                    nc.vector.tensor_copy(g4[c, t][:], ex[t][:].indirect(n4_t[:, lcols]))
-                nc.vector.tensor_tensor(nd[c, t][:, 1, :], ex[t][:].indirect(n5_t[:, lcols]), g4[c, t][:], ALU.add)
-                nc.vector.tensor_tensor(nd[c, t][:, 0, :], g3[:], ex[t][:, cols], ALU.add)
+        def fetch4(u):
+            lo, hi, t = u
+            g4[u] = ring.tile([P, hi - lo], F32, name="g4")
+            nc.vector.tensor_copy(g4[u][:], ex[t][:].indirect(listed(n4_t, lo, hi)))
+
+        fetch4(pieces[0])
+        for u, ahead in zip(pieces, pieces[1:] + [None]):
+            lo, hi, t = u
+            if ahead:
+                fetch4(ahead)
+            den[u] = keep.tile([P, hi - lo], F32, name=f"den{lo}_{t}")
+            nc.vector.tensor_tensor(den[u][:], ex[t][:].indirect(listed(n5_t, lo, hi)), g4[u][:], ALU.add)
 
         oq = keep.tile([P, S], U32, name="oq", align_bytes=64)
         osc = keep.tile([P, S], U8, name="osc", align_bytes=64)
         out_rows = out_0.rearrange("(p t) j -> p t j", t=PACK)
         words_out = out_1[0].rearrange("p n t -> p (n t)").bitcast(I32)
-        for c in range(NCH):
-            cols = slice(CH * c, CH * (c + 1))
-            y = keep.tile([P, PACK, CH], F32, name=f"y{c}")
+        back = [psum.tile([P, S], F32, name=f"bank{PACK + t}", tag=f"bank{PACK + t}") for t in range(PACK)]
+        for lo, hi in OUT_CHUNKS:
+            for jb in range(lo // P, hi // P):
+                ln_num = keep.tile([P, S], F32, name=f"ln_num{jb}")
+                nc.scalar.activation(ln_num[:], num_t[jb][:], ACT.Ln)
+                for t in range(PACK):
+                    nc.tensor.transpose(back[t][:, P * jb : P * (jb + 1)], ln_num[:, P * t : P * (t + 1)], ident[:])
+            y = keep.tile([P, PACK, hi - lo], F32, name=f"y{lo}")
             for t in range(PACK):
-                ln = ring.tile([P, 2, CH], F32, name="ln")
-                nc.scalar.activation(ln[:], nd[c, t][:], ACT.Ln)
-                nc.vector.tensor_tensor(y[:, t, :], ln[:, 0, :], ln[:, 1, :], ALU.subtract)
-            nc.sync.dma_start(out_rows[:, :, cols], y[:])
-            yi = keep.tile([P, CH * PACK], BF16, name=f"yi{c}", align_bytes=64)
-            nc.vector.tensor_copy(yi[:].rearrange("p (c i t) -> p c t i", i=4, t=PACK), y[:].rearrange("p t (c i) -> p c t i", i=4))
-            nc.vector.quantize_mx(out=oq[:, cols].bitcast(FP8X4), scales=osc[:, cols], in_=yi[:])
-            nc.sync.dma_start(words_out[:, cols], oq[:, cols].bitcast(I32))
+                ln_den = keep.tile([P, hi - lo], F32, name=f"ln_den{lo}_{t}")
+                nc.scalar.activation(ln_den[:], den[lo, hi, t][:], ACT.Ln)
+                nc.vector.tensor_tensor(y[:, t, :], back[t][:, lo:hi], ln_den[:], ALU.subtract)
+                nc.sync.dma_start(out_rows[:, t, lo:hi], y[:, t, :])
+            yi = keep.tile([P, (hi - lo) * PACK], BF16, name=f"yi{lo}", align_bytes=64)
+            interleave(nc.vector.tensor_copy, yi[:], y[:])
+            nc.vector.quantize_mx(out=oq[:, lo:hi].bitcast(FP8X4), scales=osc[:, lo:hi], in_=yi[:])
+            nc.sync.dma_start(words_out[:, lo:hi], oq[:, lo:hi].bitcast(I32))
         scales_out = out_2[0].bitcast(I32).rearrange("(q r) c -> r q c", r=4)
         for r in range(4):
             queue = nc.scalar if r % 2 else nc.sync

@@ -19,6 +19,7 @@ K, T, S, G, H = 512, 1024, 512, 2048, 512
 Z_CHUNKS = ((0, 384), (384, 512))
 Z_PIECES = (((0, 256), (256, 384)), ((384, 512),))
 HELD = {("b", (1, 2)): "zi0", ("b", (1, 3)): "zi256"}
+TURNED = (0, 1, 2)
 OUT_CHUNKS = ((0, 256), (256, 512))
 FLOPS = 2 * 2 * K * H * S
 
@@ -35,44 +36,50 @@ def tile_picked_codeoverodds_none_po_kernel(tc, x_words, x_scales, d_words, d_sc
             nc.sync.dma_start(lt[:], src)
             return lt
 
-        dsc = keep.tile([P, G], U8, name="dsc", align_bytes=64)
         xsc = keep.tile([P, T], U8, name="xsc", tag="xsc", align_bytes=64)
+        nc.gpsimd.memset(xsc[64:, :].bitcast(I32), 0)
+        x_rows = x_scales[0].bitcast(I32)
+        for q in range(2):
+            nc.scalar.dma_start(
+                xsc[32 * q : 32 * q + 32, :].bitcast(I32),
+                x_rows[4 * q : 4 * q + 4, :].unsqueeze(0).to_broadcast([8, 4, T // 4]),
+            )
+        for q in range(2, 4):
+            nc.gpsimd.dma_start(xsc[32 * q : 32 * q + 4, :].bitcast(I32), x_rows[4 * q : 4 * q + 4, :])
+        ident = keep.tile([P, P], F32, name="ident")
+        make_identity(nc, ident[:])
 
         k1_t = load_list("k1_t", k1)
-        d_rows = d_scales[0].bitcast(I32).rearrange("(g e) c -> e g c", e=2)
-        for e in range(2):
-            nc.scalar.dma_start(dsc[e:P:2, :].bitcast(I32), d_rows[e].unsqueeze(1).to_broadcast([8, 8, G // 4]))
+        dsc = keep.tile([P, G], U8, name="dsc", align_bytes=64)
+        nc.sync.dma_start(dsc[:].bitcast(I32), d_scales[0].bitcast(I32).unsqueeze(1).to_broadcast([16, 8, G // 4]))
+        k2_t = load_list("k2_t", k2)
         offs_t = load_list("offs_t", offs)
         xw = keep.tile([P, T], I32, name="xw", align_bytes=64)
         nc.sync.dma_start(xw[:], x_words[0].rearrange("p n t -> p (n t)").bitcast(I32))
         dw = keep.tile([P, G], I32, name="dw", align_bytes=64)
         nc.sync.dma_start(dw[:], d_words[0].rearrange("p n t -> p (n t)").bitcast(I32))
-        x_rows = x_scales[0].bitcast(I32).rearrange("(q r) c -> r q c", r=4)
-        for r in range(4):
-            queue = nc.scalar if r < 2 else nc.gpsimd
-            queue.dma_start(xsc[r:P:4, :].bitcast(I32), x_rows[r].unsqueeze(1).to_broadcast([4, 8, T // 4]))
         gs_t = keep.tile([P, PACK], F32, name="gs_t")
-        nc.gpsimd.dma_start(gs_t[:], gs.rearrange("(p t) o -> p (t o)", t=PACK))
-        k2_t = load_list("k2_t", k2)
+        nc.sync.dma_start(gs_t[:], gs.rearrange("(p t) o -> p (t o)", t=PACK))
         n1_t = load_list("n1_t", n1)
         n2_t = load_list("n2_t", n2)
         n3_t = load_list("n3_t", n3)
         n4_t = load_list("n4_t", n4)
         n5_t = load_list("n5_t", n5)
 
-        def pick_scales(name, lt, queue, tag):
-            got = keep.tile([P, H], U8, name=name + "_got", tag=tag, align_bytes=64)
-            nc.vector.tensor_copy(got[:], dsc[:].indirect(lt[:]))
-            dealt = keep.tile([P, H], U8, name=name, align_bytes=64)
-            nc.vector.tensor_copy(
-                dealt[:].rearrange("p (t m) -> p m t", t=PACK), got[:].rearrange("p (m t) -> p m t", t=PACK)
-            )
-            for e in range(2):
-                queue.dma_start(dealt[2 + e : P : 32, :].bitcast(I32), dealt[16 + e : P : 32, :].bitcast(I32))
-            return dealt
+        ds_got = keep.tile([P, 2 * H], U8, name="ds_got", align_bytes=64)
+        nc.vector.tensor_copy(ds_got[:, :H], dsc[:].indirect(k1_t[:]))
+        nc.vector.tensor_copy(ds_got[:, H:], dsc[:].indirect(k2_t[:]))
+        ds = keep.tile([P, 2 * H], U8, name="ds", align_bytes=64)
+        nc.vector.tensor_copy(
+            ds[:].rearrange("p (l t m) -> p l m t", l=2, t=PACK), ds_got[:].rearrange("p (l m t) -> p l m t", l=2, t=PACK)
+        )
+        for r in range(1, 4):
+            nc.scalar.dma_start(ds[r:P:32, :].bitcast(I32), ds[8 * r : P : 32, :].bitcast(I32))
+        d1s = ds[:, :H]
+        d2s = ds[:, H:]
 
-        def pick_words(name, lt, tag):
-            got = keep.tile([P, H], U32, name=name + "_got", tag=tag, align_bytes=64)
+        def pick_words(name, lt):
+            got = keep.tile([P, H], U32, name=name + "_got", tag="xsc", align_bytes=64)
             nc.vector.tensor_copy(got[:], dw[:].bitcast(U32).indirect(lt[:]))
             dealt = keep.tile([P, H], U32, name=name, align_bytes=64)
             nc.vector.tensor_copy(
@@ -80,16 +87,13 @@ def tile_picked_codeoverodds_none_po_kernel(tc, x_words, x_scales, d_words, d_sc
             )
             return dealt
 
-        d1s = pick_scales("d1s", k1_t, nc.scalar, "d1s_got")
         xg = keep.tile([P, S], U32, name="xg", align_bytes=64)
         nc.vector.tensor_copy(xg[:], xw[:].bitcast(U32).indirect(offs_t[:]))
         xs = keep.tile([P, S], U8, name="xs", align_bytes=64)
         nc.vector.tensor_copy(xs[:], xsc[:].indirect(offs_t[:]))
-        d1w = pick_words("d1w", k1_t, "d1w_got")
-        ident = keep.tile([P, P], F32, name="ident")
-        make_identity(nc, ident[:])
+        d1w = pick_words("d1w", k1_t)
         gw = keep.tile([P, PACK], F32, name="gw")
-        nc.gpsimd.tensor_scalar(gw[:], gs_t[:], 0.75 * 0.0625, 0.0, ALU.mult, ALU.add)
+        nc.scalar.activation(gw[:], gs_t[:], ACT.Copy, scale=0.75 * 0.0625)
 
         h = []
         w = []
@@ -101,12 +105,14 @@ def tile_picked_codeoverodds_none_po_kernel(tc, x_words, x_scales, d_words, d_sc
             ht = keep.tile([P, S], F32, name=f"h{t}")
             nc.scalar.activation(ht[:], acc[:], ACT.Copy, scale=0.0625)
             wt = keep.tile([P, S], F32, name=f"w{t}")
-            nc.scalar.activation(wt[:], acc[:], ACT.Copy, scale=gw[:, t : t + 1])
+            split = Z_CHUNKS[0][1] if t in TURNED else 0
+            if split:
+                nc.scalar.activation(wt[:, :split], acc[:, :split], ACT.Copy, scale=-0.75 * 0.0625)
+            nc.scalar.activation(wt[:, split:], acc[:, split:], ACT.Copy, scale=gw[:, t : t + 1])
             h.append(ht)
             w.append(wt)
 
-        d2s = pick_scales("d2s", k2_t, nc.sync, "xsc")
-        d2w = pick_words("d2w", k2_t, "d1w_got")
+        d2w = pick_words("d2w", k2_t)
 
         def listed(lt, lo, hi):
             return lt[:, lo // 16 : hi // 16]
@@ -133,6 +139,18 @@ def tile_picked_codeoverodds_none_po_kernel(tc, x_words, x_scales, d_words, d_sc
         def weigh(u):
             c, t = u
             lo, hi = Z_CHUNKS[c]
+            if c == 0 and t in TURNED:
+                there = psum.tile([P, S], F32, name="bank4", tag="bank4")
+                for j in range(lo, hi, P):
+                    nc.tensor.matmul(there[:, j : j + P], w[t][:, j : j + P], ident[:], start=True, stop=False, is_transpose=True)
+                    nc.tensor.matmul(there[:, j : j + P], m[u][:, j : j + P], ident[:], start=False, stop=True, is_transpose=True)
+                turned = ring.tile([P, hi - lo], F32, name="turned")
+                nc.scalar.copy(turned[:], there[:, lo:hi])
+                home = psum.tile([P, S], F32, name="bank5", tag="bank5")
+                for j in range(lo, hi, P):
+                    nc.tensor.transpose(home[:, j : j + P], turned[:, j : j + P], ident[:])
+                nc.scalar.activation(zb[c][:, t, :], home[:, lo:hi], ACT.Copy, scale=gs_t[:, t : t + 1])
+                return
             nc.vector.scalar_tensor_tensor(zb[c][:, t, :], m[u][:], gs_t[:, t : t + 1], w[t][:, lo:hi], ALU.mult, ALU.subtract)
 
         def interleave(copy, dst, src):
@@ -221,6 +239,7 @@ def tile_picked_codeoverodds_none_po_kernel(tc, x_words, x_scales, d_words, d_sc
         out_rows = out_0.rearrange("(p t) j -> p t j", t=PACK)
         words_out = out_1[0].rearrange("p n t -> p (n t)").bitcast(I32)
         back = [psum.tile([P, S], F32, name=f"bank{PACK + t}", tag=f"bank{PACK + t}") for t in range(PACK)]
+        ys = []
         for lo, hi in OUT_CHUNKS:
             for jb in range(lo // P, hi // P):
                 ln_num = keep.tile([P, S], F32, name=f"ln_num{jb}")
@@ -232,9 +251,12 @@ def tile_picked_codeoverodds_none_po_kernel(tc, x_words, x_scales, d_words, d_sc
                 ln_den = keep.tile([P, hi - lo], F32, name=f"ln_den{lo}_{t}")
                 nc.scalar.activation(ln_den[:], den[lo, hi, t][:], ACT.Ln)
                 nc.vector.tensor_tensor(y[:, t, :], back[t][:, lo:hi], ln_den[:], ALU.subtract)
-                nc.sync.dma_start(out_rows[:, t, lo:hi], y[:, t, :])
+                if t % 2:
+                    nc.sync.dma_start(out_rows[:, t - 1 : t + 1, lo:hi], y[:, t - 1 : t + 1, :])
+            ys.append(y)
+        for (lo, hi), y, copy in zip(OUT_CHUNKS[::-1], ys[::-1], (nc.vector.tensor_copy, nc.scalar.copy)):
             yi = keep.tile([P, (hi - lo) * PACK], BF16, name=f"yi{lo}", align_bytes=64)
-            interleave(nc.vector.tensor_copy, yi[:], y[:])
+            interleave(copy, yi[:], y[:])
             nc.vector.quantize_mx(out=oq[:, lo:hi].bitcast(FP8X4), scales=osc[:, lo:hi], in_=yi[:])
             nc.sync.dma_start(words_out[:, lo:hi], oq[:, lo:hi].bitcast(I32))
         scales_out = out_2[0].bitcast(I32).rearrange("(q r) c -> r q c", r=4)

@@ -18,7 +18,7 @@ PACK = 4
 K, T, S, G, H = 512, 1024, 512, 2048, 512
 Z_CHUNKS = ((0, 384), (384, 512))
 Z_PIECES = (((0, 256), (256, 384)), ((384, 512),))
-HELD = {("b", (1, 2)): "zi0", ("b", (1, 3)): "zi256"}
+HELD = {("b", (0, 3)): "b_last", ("b", (1, 2)): "zi0", ("b", (1, 3)): "zi256"}
 TURNED = (0, 1, 2)
 OUT_CHUNKS = ((0, 256), (256, 512))
 FLOPS = 2 * 2 * K * H * S
@@ -28,7 +28,7 @@ def tile_picked_codeoverodds_none_po_kernel(tc, x_words, x_scales, d_words, d_sc
     nc = tc.nc
     with ExitStack() as ctx:
         keep = ctx.enter_context(tc.tile_pool(name="keep", bufs=1))
-        ring = ctx.enter_context(tc.tile_pool(name="ring", bufs=3))
+        ring = ctx.enter_context(tc.tile_pool(name="ring", bufs=4))
         psum = ctx.enter_context(tc.psum_pool(name="psum", bufs=1))
 
         def load_list(name, src):
@@ -37,49 +37,45 @@ def tile_picked_codeoverodds_none_po_kernel(tc, x_words, x_scales, d_words, d_sc
             return lt
 
         xsc = keep.tile([P, T], U8, name="xsc", tag="xsc", align_bytes=64)
-        nc.gpsimd.memset(xsc[64:, :].bitcast(I32), 0)
         x_rows = x_scales[0].bitcast(I32)
-        for q in range(2):
+        for q in range(4):
             nc.scalar.dma_start(
                 xsc[32 * q : 32 * q + 32, :].bitcast(I32),
                 x_rows[4 * q : 4 * q + 4, :].unsqueeze(0).to_broadcast([8, 4, T // 4]),
             )
-        for q in range(2, 4):
-            nc.gpsimd.dma_start(xsc[32 * q : 32 * q + 4, :].bitcast(I32), x_rows[4 * q : 4 * q + 4, :])
         ident = keep.tile([P, P], F32, name="ident")
         make_identity(nc, ident[:])
 
-        k1_t = load_list("k1_t", k1)
         dsc = keep.tile([P, G], U8, name="dsc", align_bytes=64)
         nc.sync.dma_start(dsc[:].bitcast(I32), d_scales[0].bitcast(I32).unsqueeze(1).to_broadcast([16, 8, G // 4]))
-        k2_t = load_list("k2_t", k2)
+        k1_t = load_list("k1_t", k1)
         offs_t = load_list("offs_t", offs)
         xw = keep.tile([P, T], I32, name="xw", align_bytes=64)
         nc.sync.dma_start(xw[:], x_words[0].rearrange("p n t -> p (n t)").bitcast(I32))
-        dw = keep.tile([P, G], I32, name="dw", align_bytes=64)
-        nc.sync.dma_start(dw[:], d_words[0].rearrange("p n t -> p (n t)").bitcast(I32))
         gs_t = keep.tile([P, PACK], F32, name="gs_t")
         nc.sync.dma_start(gs_t[:], gs.rearrange("(p t) o -> p (t o)", t=PACK))
+        k2_t = load_list("k2_t", k2)
         n1_t = load_list("n1_t", n1)
+        dw = keep.tile([P, G], I32, name="dw", align_bytes=64)
+        nc.sync.dma_start(dw[:], d_words[0].rearrange("p n t -> p (n t)").bitcast(I32))
         n2_t = load_list("n2_t", n2)
         n3_t = load_list("n3_t", n3)
         n4_t = load_list("n4_t", n4)
         n5_t = load_list("n5_t", n5)
 
-        ds_got = keep.tile([P, 2 * H], U8, name="ds_got", align_bytes=64)
-        nc.vector.tensor_copy(ds_got[:, :H], dsc[:].indirect(k1_t[:]))
-        nc.vector.tensor_copy(ds_got[:, H:], dsc[:].indirect(k2_t[:]))
-        ds = keep.tile([P, 2 * H], U8, name="ds", align_bytes=64)
-        nc.vector.tensor_copy(
-            ds[:].rearrange("p (l t m) -> p l m t", l=2, t=PACK), ds_got[:].rearrange("p (l m t) -> p l m t", l=2, t=PACK)
-        )
-        for r in range(1, 4):
-            nc.scalar.dma_start(ds[r:P:32, :].bitcast(I32), ds[8 * r : P : 32, :].bitcast(I32))
-        d1s = ds[:, :H]
-        d2s = ds[:, H:]
+        def pick_scales(name, lt, tag, queue):
+            got = keep.tile([P, H], U8, name=name + "_got", tag=tag, align_bytes=64)
+            nc.vector.tensor_copy(got[:], dsc[:].indirect(lt[:]))
+            dealt = keep.tile([P, H], U8, name=name, align_bytes=64)
+            nc.vector.tensor_copy(
+                dealt[:].rearrange("p (t m) -> p m t", t=PACK), got[:].rearrange("p (m t) -> p m t", t=PACK)
+            )
+            for r in range(1, 4):
+                queue.dma_start(dealt[r:P:32, :].bitcast(I32), dealt[8 * r : P : 32, :].bitcast(I32))
+            return dealt
 
-        def pick_words(name, lt):
-            got = keep.tile([P, H], U32, name=name + "_got", tag="xsc", align_bytes=64)
+        def pick_words(name, lt, tag):
+            got = keep.tile([P, H], U32, name=name + "_got", tag=tag, align_bytes=64)
             nc.vector.tensor_copy(got[:], dw[:].bitcast(U32).indirect(lt[:]))
             dealt = keep.tile([P, H], U32, name=name, align_bytes=64)
             nc.vector.tensor_copy(
@@ -87,32 +83,37 @@ def tile_picked_codeoverodds_none_po_kernel(tc, x_words, x_scales, d_words, d_sc
             )
             return dealt
 
+        d1s = pick_scales("d1s", k1_t, "d1s_got", nc.scalar)
         xg = keep.tile([P, S], U32, name="xg", align_bytes=64)
         nc.vector.tensor_copy(xg[:], xw[:].bitcast(U32).indirect(offs_t[:]))
         xs = keep.tile([P, S], U8, name="xs", align_bytes=64)
         nc.vector.tensor_copy(xs[:], xsc[:].indirect(offs_t[:]))
-        d1w = pick_words("d1w", k1_t)
+        d1w = pick_words("d1w", k1_t, "xsc")
+        d2s = pick_scales("d2s", k2_t, "xsc", nc.sync)
         gw = keep.tile([P, PACK], F32, name="gw")
         nc.scalar.activation(gw[:], gs_t[:], ACT.Copy, scale=0.75 * 0.0625)
 
-        h = []
-        w = []
+        acc1 = []
         for t in range(PACK):
             acc = psum.tile([P, S], F32, name=f"bank{t}", tag=f"bank{t}")
             cols = slice(P * t, P * (t + 1))
             nc.tensor.matmul_mx(out=acc[:], lhsT=d1w[:, cols].bitcast(FP8X4), lhsT_scale=d1s[:, cols],
                                 rhs=xg[:].bitcast(FP8X4), rhs_scale=xs[:], start=True, stop=True)
-            ht = keep.tile([P, S], F32, name=f"h{t}")
-            nc.scalar.activation(ht[:], acc[:], ACT.Copy, scale=0.0625)
-            wt = keep.tile([P, S], F32, name=f"w{t}")
-            split = Z_CHUNKS[0][1] if t in TURNED else 0
-            if split:
-                nc.scalar.activation(wt[:, :split], acc[:, :split], ACT.Copy, scale=-0.75 * 0.0625)
-            nc.scalar.activation(wt[:, split:], acc[:, split:], ACT.Copy, scale=gw[:, t : t + 1])
-            h.append(ht)
-            w.append(wt)
+            acc1.append(acc)
+        h = [keep.tile([P, S], F32, name=f"h{t}") for t in range(PACK)]
+        w = [keep.tile([P, S], F32, name=f"w{t}") for t in range(PACK)]
+        split = Z_CHUNKS[0][1]
 
-        d2w = pick_words("d2w", k2_t)
+        def leave_h(t):
+            nc.scalar.activation(h[t][:], acc1[t][:], ACT.Copy, scale=0.0625)
+
+        def leave_w(t):
+            nc.scalar.activation(w[t][:, :split], acc1[t][:, :split], ACT.Copy, scale=-0.75 * 0.0625)
+
+        def leave_w_last(t):
+            lo = split if t in TURNED else 0
+            nc.scalar.activation(w[t][:, lo:], acc1[t][:, lo:], ACT.Copy, scale=gw[:, t : t + 1])
+
 
         def listed(lt, lo, hi):
             return lt[:, lo // 16 : hi // 16]
@@ -129,24 +130,33 @@ def tile_picked_codeoverodds_none_po_kernel(tc, x_words, x_scales, d_words, d_sc
                 store[u] = keep.tile([P, hi - lo], F32, name=name + "_held", tag=HELD[name, u], align_bytes=64)
             else:
                 store[u] = ring.tile([P, hi - lo], F32, name=name)
-            nc.vector.tensor_copy(store[u][:], h[u[1]][:].indirect(listed(lt, lo, hi)))
+            c, t = u
+            if c == 1 or t not in TURNED or name == "a":
+                nc.vector.tensor_copy(store[u][:], h[t][:].indirect(listed(lt, lo, hi)))
+                return
+            for plo, phi in Z_PIECES[0]:
+                nc.vector.tensor_tensor(store[u][:, plo:phi], h[t][:].indirect(listed(lt, plo, phi)), a[u][:, plo:phi], ALU.subtract)
 
         def larger(u):
             lo, hi = Z_CHUNKS[u[0]]
             m[u] = ring.tile([P, hi - lo], F32, name="m")
-            nc.vector.tensor_tensor(m[u][:], a[u][:], b[u][:], ALU.max)
+            if u[0] == 0 and u[1] in TURNED:
+                nc.scalar.activation(m[u][:], b[u][:], ACT.Relu)
+            else:
+                nc.vector.tensor_tensor(m[u][:], a[u][:], b[u][:], ALU.max)
 
         def weigh(u):
             c, t = u
             lo, hi = Z_CHUNKS[c]
             if c == 0 and t in TURNED:
-                there = psum.tile([P, S], F32, name="bank4", tag="bank4")
+                there = psum.tile([P, S], F32, name=f"bank{PACK + 2 * (t % 2)}", tag=f"bank{PACK + 2 * (t % 2)}")
                 for j in range(lo, hi, P):
                     nc.tensor.matmul(there[:, j : j + P], w[t][:, j : j + P], ident[:], start=True, stop=False, is_transpose=True)
+                    nc.tensor.matmul(there[:, j : j + P], a[u][:, j : j + P], ident[:], start=False, stop=False, is_transpose=True)
                     nc.tensor.matmul(there[:, j : j + P], m[u][:, j : j + P], ident[:], start=False, stop=True, is_transpose=True)
                 turned = ring.tile([P, hi - lo], F32, name="turned")
                 nc.scalar.copy(turned[:], there[:, lo:hi])
-                home = psum.tile([P, S], F32, name="bank5", tag="bank5")
+                home = psum.tile([P, S], F32, name=f"bank{PACK + 2 * (t % 2) + 1}", tag=f"bank{PACK + 2 * (t % 2) + 1}")
                 for j in range(lo, hi, P):
                     nc.tensor.transpose(home[:, j : j + P], turned[:, j : j + P], ident[:])
                 nc.scalar.activation(zb[c][:, t, :], home[:, lo:hi], ACT.Copy, scale=gs_t[:, t : t + 1])
@@ -156,7 +166,7 @@ def tile_picked_codeoverodds_none_po_kernel(tc, x_words, x_scales, d_words, d_sc
         def interleave(copy, dst, src):
             copy(dst.rearrange("p (c i t) -> p c t i", i=4, t=PACK), src.rearrange("p t (c i) -> p c t i", i=4))
 
-        def second_product(c):
+        def second_product(c, d2w):
             last = c == len(Z_CHUNKS) - 1
             base = Z_CHUNKS[c][0]
             first_bank = 0 if last else PACK
@@ -183,6 +193,24 @@ def tile_picked_codeoverodds_none_po_kernel(tc, x_words, x_scales, d_words, d_sc
             else:
                 nc.scalar.activation(h2[t][:, lo:hi], acc2[t][:, lo:hi], ACT.Copy, scale=0.03125)
 
+        leave_h(0)
+        leave_h(1)
+        leave_w(0)
+        leave_h(2)
+        leave_w(1)
+        fetch(a, "a", n1_t, (0, 0))
+        for t in TURNED:
+            if t + 1 in TURNED:
+                fetch(a, "a", n1_t, (0, t + 1))
+            fetch(b, "b", n2_t, (0, t))
+            larger((0, t))
+            if t == 0:
+                leave_h(3)
+                leave_w(2)
+            weigh((0, t))
+        for t in reversed(range(PACK)):
+            leave_w_last(t)
+        units = units[len(TURNED) :]
         fetch(a, "a", n1_t, units[0])
         fetch(b, "b", n2_t, units[0])
         for u, ahead in zip(units, units[1:] + [None]):
@@ -193,10 +221,11 @@ def tile_picked_codeoverodds_none_po_kernel(tc, x_words, x_scales, d_words, d_sc
                 fetch(b, "b", n2_t, ahead)
             weigh(u)
             if u == (0, PACK - 1):
-                early = second_product(0)
+                d2w = pick_words("d2w", k2_t, "b_last")
+                early = second_product(0, d2w)
                 raw_second(early, 0, 0, False)
                 raw_second(early, 0, 1, False)
-        late = second_product(1)
+        late = second_product(1, d2w)
         raw_second(early, 0, 2, True)
         raw_second(early, 0, 3, True)
         for t in range(PACK):

from contextlib import ExitStack

import concourse.mybir as mybir
from concourse.masks import make_identity

F32 = mybir.dt.float32
BF16 = mybir.dt.bfloat16
I32 = mybir.dt.int32
U32 = mybir.dt.uint32
U16 = mybir.dt.uint16
U8 = mybir.dt.uint8
FP8X4 = mybir.dt.float8_e4m3fn_x4
ALU = mybir.AluOpType
ACT = mybir.ActivationFunctionType

P = 128
PACK = 4
K, T, S, G, H = 512, 1024, 512, 2048, 512
Z_CHUNKS = ((0, 384), (384, 512))
Z_PIECES = (((0, 256), (256, 384)), ((384, 512),))
HELD = {("b", (0, 3)): "b_last", ("b", (1, 2)): "zi0", ("b", (1, 3)): "zi256"}
TURNED = (0, 1, 2)
OUT_CHUNKS = ((0, 256), (256, 512))
FLOPS = 2 * 2 * K * H * S


def tile_picked_codeoverodds_none_po_kernel(tc, x_words, x_scales, d_words, d_scales, gs, offs, k1, n1, n2, k2, n3, n4, n5, out_0, out_1, out_2):
    nc = tc.nc
    with ExitStack() as ctx:
        keep = ctx.enter_context(tc.tile_pool(name="keep", bufs=1))
        ring = ctx.enter_context(tc.tile_pool(name="ring", bufs=4))
        psum = ctx.enter_context(tc.psum_pool(name="psum", bufs=1))

        def load_list(name, src):
            lt = keep.tile([P, S // 16], U16, name=name)
            nc.sync.dma_start(lt[:], src)
            return lt

        xsc = keep.tile([P, T], U8, name="xsc", tag="xsc", align_bytes=64)
        x_rows = x_scales[0].bitcast(I32)
        for q in range(4):
            nc.scalar.dma_start(
                xsc[32 * q : 32 * q + 32, :].bitcast(I32),
                x_rows[4 * q : 4 * q + 4, :].unsqueeze(0).to_broadcast([8, 4, T // 4]),
            )
        ident = keep.tile([P, P], F32, name="ident")
        make_identity(nc, ident[:])

        dsc = keep.tile([P, G], U8, name="dsc", align_bytes=64)
        nc.sync.dma_start(dsc[:].bitcast(I32), d_scales[0].bitcast(I32).unsqueeze(1).to_broadcast([16, 8, G // 4]))
        k1_t = load_list("k1_t", k1)
        offs_t = load_list("offs_t", offs)
        xw = keep.tile([P, T], I32, name="xw", align_bytes=64)
        nc.sync.dma_start(xw[:], x_words[0].rearrange("p n t -> p (n t)").bitcast(I32))
        gs_t = keep.tile([P, PACK], F32, name="gs_t")
        nc.sync.dma_start(gs_t[:], gs.rearrange("(p t) o -> p (t o)", t=PACK))
        k2_t = load_list("k2_t", k2)
        n1_t = load_list("n1_t", n1)
        dw = keep.tile([P, G], I32, name="dw", align_bytes=64)
        nc.sync.dma_start(dw[:], d_words[0].rearrange("p n t -> p (n t)").bitcast(I32))
        n2_t = load_list("n2_t", n2)
        n3_t = load_list("n3_t", n3)
        n4_t = load_list("n4_t", n4)
        n5_t = load_list("n5_t", n5)

        def pick_scales(name, lt, tag, queue):
            got = keep.tile([P, H], U8, name=name + "_got", tag=tag, align_bytes=64)
            nc.vector.tensor_copy(got[:], dsc[:].indirect(lt[:]))
            dealt = keep.tile([P, H], U8, name=name, align_bytes=64)
            nc.vector.tensor_copy(
                dealt[:].rearrange("p (t m) -> p m t", t=PACK), got[:].rearrange("p (m t) -> p m t", t=PACK)
            )
            for r in range(1, 4):
                queue.dma_start(dealt[r:P:32, :].bitcast(I32), dealt[8 * r : P : 32, :].bitcast(I32))
            return dealt

        def pick_words(name, lt, tag):
            got = keep.tile([P, H], U32, name=name + "_got", tag=tag, align_bytes=64)
            nc.vector.tensor_copy(got[:], dw[:].bitcast(U32).indirect(lt[:]))
            dealt = keep.tile([P, H], U32, name=name, align_bytes=64)
            nc.vector.tensor_copy(
                dealt[:].rearrange("p (t m) -> p m t", t=PACK), got[:].rearrange("p (m t) -> p m t", t=PACK)
            )
            return dealt

        d1s = pick_scales("d1s", k1_t, "d1s_got", nc.scalar)
        xg = keep.tile([P, S], U32, name="xg", align_bytes=64)
        nc.vector.tensor_copy(xg[:], xw[:].bitcast(U32).indirect(offs_t[:]))
        xs = keep.tile([P, S], U8, name="xs", align_bytes=64)
        nc.vector.tensor_copy(xs[:], xsc[:].indirect(offs_t[:]))
        d1w = pick_words("d1w", k1_t, "xsc")
        d2s = pick_scales("d2s", k2_t, "xsc", nc.sync)
        gw = keep.tile([P, PACK], F32, name="gw")
        nc.scalar.activation(gw[:], gs_t[:], ACT.Copy, scale=0.75 * 0.0625)

        acc1 = []
        for t in range(PACK):
            acc = psum.tile([P, S], F32, name=f"bank{t}", tag=f"bank{t}")
            cols = slice(P * t, P * (t + 1))
            nc.tensor.matmul_mx(out=acc[:], lhsT=d1w[:, cols].bitcast(FP8X4), lhsT_scale=d1s[:, cols],
                                rhs=xg[:].bitcast(FP8X4), rhs_scale=xs[:], start=True, stop=True)
            acc1.append(acc)
        h = [keep.tile([P, S], F32, name=f"h{t}") for t in range(PACK)]
        w = [keep.tile([P, S], F32, name=f"w{t}") for t in range(PACK)]
        split = Z_CHUNKS[0][1]

        def leave_h(t):
            nc.scalar.activation(h[t][:], acc1[t][:], ACT.Copy, scale=0.0625)

        def leave_w(t):
            nc.scalar.activation(w[t][:, :split], acc1[t][:, :split], ACT.Copy, scale=-0.75 * 0.0625)

        def leave_w_last(t):
            lo = split if t in TURNED else 0
            nc.scalar.activation(w[t][:, lo:], acc1[t][:, lo:], ACT.Copy, scale=gw[:, t : t + 1])


        def listed(lt, lo, hi):
            return lt[:, lo // 16 : hi // 16]

        ex = [keep.tile([P, S], F32, name=f"ex{t}") for t in range(PACK)]
        h2 = [keep.tile([P, S], F32, name=f"h2_{t}") for t in range(PACK)]
        zb = [keep.tile([P, PACK, hi - lo], BF16, name=f"zb{lo}", align_bytes=64) for lo, hi in Z_CHUNKS]
        units = [(c, t) for c in range(len(Z_CHUNKS)) for t in range(PACK)]
        a, b, m = {}, {}, {}

        def fetch(store, name, lt, u):
            lo, hi = Z_CHUNKS[u[0]]
            if (name, u) in HELD:
                store[u] = keep.tile([P, hi - lo], F32, name=name + "_held", tag=HELD[name, u], align_bytes=64)
            else:
                store[u] = ring.tile([P, hi - lo], F32, name=name)
            c, t = u
            if c == 1 or t not in TURNED or name == "a":
                nc.vector.tensor_copy(store[u][:], h[t][:].indirect(listed(lt, lo, hi)))
                return
            for plo, phi in Z_PIECES[0]:
                nc.vector.tensor_tensor(store[u][:, plo:phi], h[t][:].indirect(listed(lt, plo, phi)), a[u][:, plo:phi], ALU.subtract)

        def larger(u):
            lo, hi = Z_CHUNKS[u[0]]
            m[u] = ring.tile([P, hi - lo], F32, name="m")
            if u[0] == 0 and u[1] in TURNED:
                nc.scalar.activation(m[u][:], b[u][:], ACT.Relu)
            else:
                nc.vector.tensor_tensor(m[u][:], a[u][:], b[u][:], ALU.max)

        def weigh(u):
            c, t = u
            lo, hi = Z_CHUNKS[c]
            if c == 0 and t in TURNED:
                there = psum.tile([P, S], F32, name=f"bank{PACK + 2 * (t % 2)}", tag=f"bank{PACK + 2 * (t % 2)}")
                for j in range(lo, hi, P):
                    nc.tensor.matmul(there[:, j : j + P], w[t][:, j : j + P], ident[:], start=True, stop=False, is_transpose=True)
                    nc.tensor.matmul(there[:, j : j + P], a[u][:, j : j + P], ident[:], start=False, stop=False, is_transpose=True)
                    nc.tensor.matmul(there[:, j : j + P], m[u][:, j : j + P], ident[:], start=False, stop=True, is_transpose=True)
                turned = ring.tile([P, hi - lo], F32, name="turned")
                nc.scalar.copy(turned[:], there[:, lo:hi])
                home = psum.tile([P, S], F32, name=f"bank{PACK + 2 * (t % 2) + 1}", tag=f"bank{PACK + 2 * (t % 2) + 1}")
                for j in range(lo, hi, P):
                    nc.tensor.transpose(home[:, j : j + P], turned[:, j : j + P], ident[:])
                nc.scalar.activation(zb[c][:, t, :], home[:, lo:hi], ACT.Copy, scale=gs_t[:, t : t + 1])
                return
            nc.vector.scalar_tensor_tensor(zb[c][:, t, :], m[u][:], gs_t[:, t : t + 1], w[t][:, lo:hi], ALU.mult, ALU.subtract)

        def interleave(copy, dst, src):
            copy(dst.rearrange("p (c i t) -> p c t i", i=4, t=PACK), src.rearrange("p t (c i) -> p c t i", i=4))

        def second_product(c, d2w):
            last = c == len(Z_CHUNKS) - 1
            base = Z_CHUNKS[c][0]
            first_bank = 0 if last else PACK
            acc2 = [psum.tile([P, S], F32, name=f"bank{first_bank + t}", tag=f"bank{first_bank + t}") for t in range(PACK)]
            for lo, hi in Z_PIECES[c]:
                zi = keep.tile([P, (hi - lo) * PACK], BF16, name=f"zi{lo}", tag=f"zi{lo}", align_bytes=64)
                interleave(nc.vector.tensor_copy if last else nc.scalar.copy, zi[:], zb[c][:, :, lo - base : hi - base])
                zq = keep.tile([P, hi - lo], U32, name=f"zq{lo}", align_bytes=64)
                zs = keep.tile([P, hi - lo], U8, name=f"zs{lo}", align_bytes=64)
                nc.vector.quantize_mx(out=zq[:].bitcast(FP8X4), scales=zs[:], in_=zi[:])
                for t in range(PACK):
                    mcols = slice(P * t, P * (t + 1))
                    nc.tensor.matmul_mx(out=acc2[t][:, lo:hi], lhsT=d2w[:, mcols].bitcast(FP8X4), lhsT_scale=d2s[:, mcols],
                                        rhs=zq[:].bitcast(FP8X4), rhs_scale=zs[:], start=True, stop=True)
            lo, hi = Z_CHUNKS[c]
            for t in range(PACK):
                nc.scalar.activation(ex[t][:, lo:hi], acc2[t][:, lo:hi], ACT.Exp, scale=0.03125)
            return acc2

        def raw_second(acc2, c, t, on_vector):
            lo, hi = Z_CHUNKS[c]
            if on_vector:
                nc.vector.tensor_scalar_mul(h2[t][:, lo:hi], acc2[t][:, lo:hi], 0.03125)
            else:
                nc.scalar.activation(h2[t][:, lo:hi], acc2[t][:, lo:hi], ACT.Copy, scale=0.03125)

        leave_h(0)
        leave_h(1)
        leave_w(0)
        leave_h(2)
        leave_w(1)
        fetch(a, "a", n1_t, (0, 0))
        for t in TURNED:
            if t + 1 in TURNED:
                fetch(a, "a", n1_t, (0, t + 1))
            fetch(b, "b", n2_t, (0, t))
            larger((0, t))
            if t == 0:
                leave_h(3)
                leave_w(2)
            weigh((0, t))
        for t in reversed(range(PACK)):
            leave_w_last(t)
        units = units[len(TURNED) :]
        fetch(a, "a", n1_t, units[0])
        fetch(b, "b", n2_t, units[0])
        for u, ahead in zip(units, units[1:] + [None]):
            if ahead:
                fetch(a, "a", n1_t, ahead)
            larger(u)
            if ahead:
                fetch(b, "b", n2_t, ahead)
            weigh(u)
            if u == (0, PACK - 1):
                d2w = pick_words("d2w", k2_t, "b_last")
                early = second_product(0, d2w)
                raw_second(early, 0, 0, False)
                raw_second(early, 0, 1, False)
        late = second_product(1, d2w)
        raw_second(early, 0, 2, True)
        raw_second(early, 0, 3, True)
        for t in range(PACK):
            raw_second(late, 1, t, False)

        g3 = [keep.tile([P, S], F32, name=f"g3_{t}") for t in range(PACK)]
        for lo in range(0, S, 256):
            for t in range(PACK):
                nc.scalar.activation(g3[t][:, lo : lo + 256], h2[t][:].indirect(listed(n3_t, lo, lo + 256)), ACT.Exp)

        num_t = []
        for jb in range(S // P):
            bank = psum.tile([P, S], F32, name=f"bank{jb}", tag=f"bank{jb}")
            jcols = slice(P * jb, P * (jb + 1))
            for t in range(PACK):
                mcols = slice(P * t, P * (t + 1))
                nc.tensor.matmul(bank[:, mcols], ex[t][:, jcols], ident[:], start=True, stop=False, is_transpose=True)
                nc.tensor.matmul(bank[:, mcols], g3[t][:, jcols], ident[:], start=False, stop=True, is_transpose=True)
            num_t.append(bank)

        den = {}
        g4 = {}
        pieces = [(lo, hi, t) for lo, hi in OUT_CHUNKS for t in range(PACK)]

        def fetch4(u):
            lo, hi, t = u
            g4[u] = ring.tile([P, hi - lo], F32, name="g4")
            nc.vector.tensor_copy(g4[u][:], ex[t][:].indirect(listed(n4_t, lo, hi)))

        fetch4(pieces[0])
        for u, ahead in zip(pieces, pieces[1:] + [None]):
            lo, hi, t = u
            if ahead:
                fetch4(ahead)
            den[u] = keep.tile([P, hi - lo], F32, name=f"den{lo}_{t}")
            nc.vector.tensor_tensor(den[u][:], ex[t][:].indirect(listed(n5_t, lo, hi)), g4[u][:], ALU.add)

        oq = keep.tile([P, S], U32, name="oq", align_bytes=64)
        osc = keep.tile([P, S], U8, name="osc", align_bytes=64)
        out_rows = out_0.rearrange("(p t) j -> p t j", t=PACK)
        words_out = out_1[0].rearrange("p n t -> p (n t)").bitcast(I32)
        back = [psum.tile([P, S], F32, name=f"bank{PACK + t}", tag=f"bank{PACK + t}") for t in range(PACK)]
        ys = []
        for lo, hi in OUT_CHUNKS:
            for jb in range(lo // P, hi // P):
                ln_num = keep.tile([P, S], F32, name=f"ln_num{jb}")
                nc.scalar.activation(ln_num[:], num_t[jb][:], ACT.Ln)
                for t in range(PACK):
                    nc.tensor.transpose(back[t][:, P * jb : P * (jb + 1)], ln_num[:, P * t : P * (t + 1)], ident[:])
            y = keep.tile([P, PACK, hi - lo], F32, name=f"y{lo}")
            for t in range(PACK):
                ln_den = keep.tile([P, hi - lo], F32, name=f"ln_den{lo}_{t}")
                nc.scalar.activation(ln_den[:], den[lo, hi, t][:], ACT.Ln)
                nc.vector.tensor_tensor(y[:, t, :], back[t][:, lo:hi], ln_den[:], ALU.subtract)
                if t % 2:
                    nc.sync.dma_start(out_rows[:, t - 1 : t + 1, lo:hi], y[:, t - 1 : t + 1, :])
            ys.append(y)
        for (lo, hi), y, copy in zip(OUT_CHUNKS[::-1], ys[::-1], (nc.vector.tensor_copy, nc.scalar.copy)):
            yi = keep.tile([P, (hi - lo) * PACK], BF16, name=f"yi{lo}", align_bytes=64)
            interleave(copy, yi[:], y[:])
            nc.vector.quantize_mx(out=oq[:, lo:hi].bitcast(FP8X4), scales=osc[:, lo:hi], in_=yi[:])
            nc.sync.dma_start(words_out[:, lo:hi], oq[:, lo:hi].bitcast(I32))
        scales_out = out_2[0].bitcast(I32).rearrange("(q r) c -> r q c", r=4)
        for r in range(4):
            queue = nc.scalar if r % 2 else nc.sync
            queue.dma_start(scales_out[r], osc[r:P:32, :].bitcast(I32))
